import numpy as np
import ml_dtypes

BF16 = ml_dtypes.bfloat16


def bf(x):
    return np.asarray(x, np.float32).astype(BF16)


def f32(x):
    return np.asarray(x, np.float32)


def f64(x):
    return np.asarray(x).astype(np.float64)


def striped(idx):
    return np.tile(idx.reshape(-1, 16).T, (8, 1))


def rows(idx, k):
    return np.tile(idx, (k, 1))


def look(tab, idx):
    return np.take_along_axis(f64(tab), rows(idx, len(tab)), axis=1)


K, S, V, N = 128, 2048, 512, 512


def silu(v):
    return v / (1.0 + np.exp(-v))


def setup_inputs():
    return {"tab": f32(np.random.standard_normal((2, K, S))), "y": f32(np.random.standard_normal((K, V))), "offs": striped(np.random.permutation(S)[:N])}


def reference(tab, y, offs):
    idx = offs[:16].T.reshape(-1)
    x = (np.minimum(look(tab[0], idx), f64(y))) * (silu(look(tab[1], idx)))
    return x

@@ -1,0 +1,43 @@
+import concourse.mybir as mybir
+
+F32 = mybir.dt.float32
+U16 = mybir.dt.uint16
+MIN = mybir.AluOpType.min
+MULT = mybir.AluOpType.mult
+SILU = mybir.ActivationFunctionType.Silu
+
+ROWS, PLACES, PICKS = 128, 2048, 512
+
+PIECE = PICKS // 2
+
+FLOPS = 6 * ROWS * PICKS
+
+
+def tile_lookup_vg_minsilu_out_kernel(tc, tab, y, offs, out):
+    nc = tc.nc
+    with tc.tile_pool(name="held", bufs=1) as held:
+        offsets = held.tile([ROWS, PICKS // 16], U16, name="offsets")
+        gates = held.tile([ROWS, PLACES], F32, name="gates")
+        values = held.tile([ROWS, PLACES], F32, name="values")
+        stream = held.tile([ROWS, PICKS], F32, name="stream")
+        gated = held.tile([ROWS, PICKS], F32, name="gated")
+        lesser = held.tile([ROWS, PICKS], F32, name="lesser")
+        product = held.tile([ROWS, PICKS], F32, name="product")
+
+        zeros = held.tile([ROWS, 1], F32, name="zeros")
+        warmed = held.tile([ROWS, 1], F32, name="warmed")
+        nc.vector.memset(zeros[:], 0.0)
+        nc.scalar.activation(warmed[:], zeros[:], SILU)
+
+        nc.sync.dma_start(offsets[:], offs)
+        nc.sync.dma_start(gates[:], tab[1])
+        nc.sync.dma_start(stream[:], y)
+        nc.sync.dma_start(values[:], tab[0])
+
+        nc.scalar.activation(gated[:], gates[:].indirect(offsets[:]), SILU)
+        for first in range(0, PICKS, PIECE):
+            piece = slice(first, first + PIECE)
+            piece_offsets = offsets[:, first // 16 : (first + PIECE) // 16]
+            nc.vector.tensor_tensor(lesser[:, piece], values[:].indirect(piece_offsets), stream[:, piece], MIN)
+            nc.vector.tensor_tensor(product[:, piece], lesser[:, piece], gated[:, piece], MULT)
+            nc.sync.dma_start(out[:, piece], product[:, piece])

@@ -7,16 +7,18 @@ MULT = mybir.AluOpType.mult
 SILU = mybir.ActivationFunctionType.Silu
 
 ROWS, PLACES, PICKS = 128, 2048, 512
-
-PIECE = PICKS // 2
+PER_COLUMN = 16
 
 FLOPS = 6 * ROWS * PICKS
+
+HALF = PICKS // 2
+EARLY = 192
 
 
 def tile_lookup_vg_minsilu_out_kernel(tc, tab, y, offs, out):
     nc = tc.nc
     with tc.tile_pool(name="held", bufs=1) as held:
-        offsets = held.tile([ROWS, PICKS // 16], U16, name="offsets")
+        offsets = held.tile([ROWS, PICKS // PER_COLUMN], U16, name="offsets")
         gates = held.tile([ROWS, PLACES], F32, name="gates")
         values = held.tile([ROWS, PLACES], F32, name="values")
         stream = held.tile([ROWS, PICKS], F32, name="stream")
@@ -24,20 +26,17 @@ def tile_lookup_vg_minsilu_out_kernel(tc, tab, y, offs, out):
         lesser = held.tile([ROWS, PICKS], F32, name="lesser")
         product = held.tile([ROWS, PICKS], F32, name="product")
 
-        zeros = held.tile([ROWS, 1], F32, name="zeros")
-        warmed = held.tile([ROWS, 1], F32, name="warmed")
-        nc.vector.memset(zeros[:], 0.0)
-        nc.scalar.activation(warmed[:], zeros[:], SILU)
-
-        nc.sync.dma_start(offsets[:], offs)
         nc.sync.dma_start(gates[:], tab[1])
-        nc.sync.dma_start(stream[:], y)
+        nc.sync.dma_start(offsets[:], offs)
+        nc.sync.dma_start(stream[:, :EARLY], y[:, :EARLY])
         nc.sync.dma_start(values[:], tab[0])
+        nc.sync.dma_start(stream[:, EARLY:], y[:, EARLY:])
 
         nc.scalar.activation(gated[:], gates[:].indirect(offsets[:]), SILU)
-        for first in range(0, PICKS, PIECE):
-            piece = slice(first, first + PIECE)
-            piece_offsets = offsets[:, first // 16 : (first + PIECE) // 16]
-            nc.vector.tensor_tensor(lesser[:, piece], values[:].indirect(piece_offsets), stream[:, piece], MIN)
-            nc.vector.tensor_tensor(product[:, piece], lesser[:, piece], gated[:, piece], MULT)
-            nc.sync.dma_start(out[:, piece], product[:, piece])
+        for first, last in ((0, EARLY), (EARLY, HALF), (HALF, PICKS)):
+            piece_offsets = offsets[:, first // PER_COLUMN : last // PER_COLUMN]
+            nc.vector.tensor_tensor(lesser[:, first:last], values[:].indirect(piece_offsets), stream[:, first:last], MIN)
+        for first in (0, HALF):
+            half = slice(first, first + HALF)
+            nc.vector.tensor_tensor(product[:, half], lesser[:, half], gated[:, half], MULT)
+            nc.sync.dma_start(out[:, half], product[:, half])

@@ -26,11 +26,11 @@ def tile_lookup_vg_minsilu_out_kernel(tc, tab, y, offs, out):
         lesser = held.tile([ROWS, PICKS], F32, name="lesser")
         product = held.tile([ROWS, PICKS], F32, name="product")
 
-        nc.sync.dma_start(gates[:], tab[1])
+        nc.scalar.dma_start(gates[:], tab[1])
         nc.sync.dma_start(offsets[:], offs)
         nc.sync.dma_start(stream[:, :EARLY], y[:, :EARLY])
-        nc.sync.dma_start(values[:], tab[0])
-        nc.sync.dma_start(stream[:, EARLY:], y[:, EARLY:])
+        nc.scalar.dma_start(values[:], tab[0])
+        nc.scalar.dma_start(stream[:, EARLY:], y[:, EARLY:])
 
         nc.scalar.activation(gated[:], gates[:].indirect(offsets[:]), SILU)
         for first, last in ((0, EARLY), (EARLY, HALF), (HALF, PICKS)):

@@ -12,7 +12,7 @@ PER_COLUMN = 16
 FLOPS = 6 * ROWS * PICKS
 
 HALF = PICKS // 2
-EARLY = 192
+EARLY = 128
 
 
 def tile_lookup_vg_minsilu_out_kernel(tc, tab, y, offs, out):

@@ -22,17 +22,19 @@ def tile_lookup_vg_minsilu_out_kernel(tc, tab, y, offs, out):
         gates = held.tile([ROWS, PLACES], F32, name="gates")
         values = held.tile([ROWS, PLACES], F32, name="values")
         stream = held.tile([ROWS, PICKS], F32, name="stream")
+        landed = held.tile([ROWS, EARLY], F32, name="landed")
         gated = held.tile([ROWS, PICKS], F32, name="gated")
         lesser = held.tile([ROWS, PICKS], F32, name="lesser")
         product = held.tile([ROWS, PICKS], F32, name="product")
 
         nc.scalar.dma_start(gates[:], tab[1])
+        nc.sync.dma_start(landed[:], y[:, :EARLY])
         nc.sync.dma_start(offsets[:], offs)
-        nc.sync.dma_start(stream[:, :EARLY], y[:, :EARLY])
         nc.scalar.dma_start(values[:], tab[0])
         nc.scalar.dma_start(stream[:, EARLY:], y[:, EARLY:])
 
         nc.scalar.activation(gated[:], gates[:].indirect(offsets[:]), SILU)
+        nc.vector.tensor_copy(stream[:, :EARLY], landed[:])
         for first, last in ((0, EARLY), (EARLY, HALF), (HALF, PICKS)):
             piece_offsets = offsets[:, first // PER_COLUMN : last // PER_COLUMN]
             nc.vector.tensor_tensor(lesser[:, first:last], values[:].indirect(piece_offsets), stream[:, first:last], MIN)

@@ -13,28 +13,27 @@ FLOPS = 6 * ROWS * PICKS
 
 HALF = PICKS // 2
 EARLY = 128
+DMA_ALIGN = 256
 
 
 def tile_lookup_vg_minsilu_out_kernel(tc, tab, y, offs, out):
     nc = tc.nc
     with tc.tile_pool(name="held", bufs=1) as held:
         offsets = held.tile([ROWS, PICKS // PER_COLUMN], U16, name="offsets")
-        gates = held.tile([ROWS, PLACES], F32, name="gates")
-        values = held.tile([ROWS, PLACES], F32, name="values")
-        stream = held.tile([ROWS, PICKS], F32, name="stream")
-        landed = held.tile([ROWS, EARLY], F32, name="landed")
+        gates = held.tile([ROWS, PLACES], F32, name="gates", align_bytes=DMA_ALIGN)
+        values = held.tile([ROWS, PLACES], F32, name="values", align_bytes=DMA_ALIGN)
+        stream = held.tile([ROWS, PICKS], F32, name="stream", align_bytes=DMA_ALIGN)
         gated = held.tile([ROWS, PICKS], F32, name="gated")
         lesser = held.tile([ROWS, PICKS], F32, name="lesser")
-        product = held.tile([ROWS, PICKS], F32, name="product")
+        product = held.tile([ROWS, PICKS], F32, name="product", align_bytes=DMA_ALIGN)
 
-        nc.scalar.dma_start(gates[:], tab[1])
-        nc.sync.dma_start(landed[:], y[:, :EARLY])
+        nc.sync.dma_start(gates[:], tab[1])
+        nc.scalar.dma_start(stream[:, :EARLY], y[:, :EARLY])
         nc.sync.dma_start(offsets[:], offs)
-        nc.scalar.dma_start(values[:], tab[0])
-        nc.scalar.dma_start(stream[:, EARLY:], y[:, EARLY:])
+        nc.sync.dma_start(values[:], tab[0])
+        nc.sync.dma_start(stream[:, EARLY:], y[:, EARLY:])
 
         nc.scalar.activation(gated[:], gates[:].indirect(offsets[:]), SILU)
-        nc.vector.tensor_copy(stream[:, :EARLY], landed[:])
         for first, last in ((0, EARLY), (EARLY, HALF), (HALF, PICKS)):
             piece_offsets = offsets[:, first // PER_COLUMN : last // PER_COLUMN]
             nc.vector.tensor_tensor(lesser[:, first:last], values[:].indirect(piece_offsets), stream[:, first:last], MIN)

@@ -13,13 +13,13 @@ FLOPS = 6 * ROWS * PICKS
 
 HALF = PICKS // 2
 EARLY = 128
-DMA_ALIGN = 256
+DMA_ALIGN = 4096
 
 
 def tile_lookup_vg_minsilu_out_kernel(tc, tab, y, offs, out):
     nc = tc.nc
     with tc.tile_pool(name="held", bufs=1) as held:
-        offsets = held.tile([ROWS, PICKS // PER_COLUMN], U16, name="offsets")
+        offsets = held.tile([ROWS, PICKS // PER_COLUMN], U16, name="offsets", align_bytes=DMA_ALIGN)
         gates = held.tile([ROWS, PLACES], F32, name="gates", align_bytes=DMA_ALIGN)
         values = held.tile([ROWS, PLACES], F32, name="values", align_bytes=DMA_ALIGN)
         stream = held.tile([ROWS, PICKS], F32, name="stream", align_bytes=DMA_ALIGN)

@@ -10,10 +10,11 @@ ROWS, PLACES, PICKS = 128, 2048, 512
 PER_COLUMN = 16
 
 FLOPS = 6 * ROWS * PICKS
+DMA_ALIGN = 4096
 
 HALF = PICKS // 2
 EARLY = 128
-DMA_ALIGN = 4096
+LAST = 64
 
 
 def tile_lookup_vg_minsilu_out_kernel(tc, tab, y, offs, out):
@@ -27,6 +28,16 @@ def tile_lookup_vg_minsilu_out_kernel(tc, tab, y, offs, out):
         lesser = held.tile([ROWS, PICKS], F32, name="lesser")
         product = held.tile([ROWS, PICKS], F32, name="product", align_bytes=DMA_ALIGN)
 
+        def look_up(first, last):
+            piece_offsets = offsets[:, first // PER_COLUMN : last // PER_COLUMN]
+            nc.vector.tensor_tensor(lesser[:, first:last], values[:].indirect(piece_offsets), stream[:, first:last], MIN)
+
+        def multiply(first, last):
+            nc.vector.tensor_tensor(product[:, first:last], lesser[:, first:last], gated[:, first:last], MULT)
+
+        def store(first, last):
+            nc.sync.dma_start(out[:, first:last], product[:, first:last])
+
         nc.sync.dma_start(gates[:], tab[1])
         nc.scalar.dma_start(stream[:, :EARLY], y[:, :EARLY])
         nc.sync.dma_start(offsets[:], offs)
@@ -34,10 +45,13 @@ def tile_lookup_vg_minsilu_out_kernel(tc, tab, y, offs, out):
         nc.sync.dma_start(stream[:, EARLY:], y[:, EARLY:])
 
         nc.scalar.activation(gated[:], gates[:].indirect(offsets[:]), SILU)
-        for first, last in ((0, EARLY), (EARLY, HALF), (HALF, PICKS)):
-            piece_offsets = offsets[:, first // PER_COLUMN : last // PER_COLUMN]
-            nc.vector.tensor_tensor(lesser[:, first:last], values[:].indirect(piece_offsets), stream[:, first:last], MIN)
-        for first in (0, HALF):
-            half = slice(first, first + HALF)
-            nc.vector.tensor_tensor(product[:, half], lesser[:, half], gated[:, half], MULT)
-            nc.sync.dma_start(out[:, half], product[:, half])
+
+        look_up(0, EARLY)
+        look_up(EARLY, HALF)
+        look_up(HALF, PICKS - LAST)
+        multiply(0, HALF)
+        store(0, HALF)
+        look_up(PICKS - LAST, PICKS)
+        multiply(HALF, PICKS - LAST)
+        multiply(PICKS - LAST, PICKS)
+        store(HALF, PICKS)

@@ -12,9 +12,9 @@ PER_COLUMN = 16
 FLOPS = 6 * ROWS * PICKS
 DMA_ALIGN = 4096
 
-HALF = PICKS // 2
-EARLY = 128
-LAST = 64
+QUARTER = PICKS // 4
+EARLY = 192
+FIRST = 160
 
 
 def tile_lookup_vg_minsilu_out_kernel(tc, tab, y, offs, out):
@@ -24,34 +24,33 @@ def tile_lookup_vg_minsilu_out_kernel(tc, tab, y, offs, out):
         gates = held.tile([ROWS, PLACES], F32, name="gates", align_bytes=DMA_ALIGN)
         values = held.tile([ROWS, PLACES], F32, name="values", align_bytes=DMA_ALIGN)
         stream = held.tile([ROWS, PICKS], F32, name="stream", align_bytes=DMA_ALIGN)
+        landed = held.tile([ROWS, EARLY], F32, name="landed", align_bytes=DMA_ALIGN)
         gated = held.tile([ROWS, PICKS], F32, name="gated")
         lesser = held.tile([ROWS, PICKS], F32, name="lesser")
         product = held.tile([ROWS, PICKS], F32, name="product", align_bytes=DMA_ALIGN)
 
-        def look_up(first, last):
+        def look_up(first, last, columns):
             piece_offsets = offsets[:, first // PER_COLUMN : last // PER_COLUMN]
-            nc.vector.tensor_tensor(lesser[:, first:last], values[:].indirect(piece_offsets), stream[:, first:last], MIN)
+            nc.vector.tensor_tensor(lesser[:, first:last], values[:].indirect(piece_offsets), columns[:, first:last], MIN)
 
-        def multiply(first, last):
-            nc.vector.tensor_tensor(product[:, first:last], lesser[:, first:last], gated[:, first:last], MULT)
+        def outer(rows):
+            return rows.rearrange("p (q c) -> p q c", c=QUARTER)[:, ::3, :]
 
-        def store(first, last):
-            nc.sync.dma_start(out[:, first:last], product[:, first:last])
+        def middle(rows):
+            return rows[:, QUARTER : PICKS - QUARTER]
 
         nc.sync.dma_start(gates[:], tab[1])
-        nc.scalar.dma_start(stream[:, :EARLY], y[:, :EARLY])
+        nc.scalar.dma_start(landed[:], y[:, :EARLY])
+        nc.scalar.dma_start(values[:], tab[0])
         nc.sync.dma_start(offsets[:], offs)
-        nc.sync.dma_start(values[:], tab[0])
-        nc.sync.dma_start(stream[:, EARLY:], y[:, EARLY:])
+        nc.scalar.dma_start(stream[:, EARLY:], y[:, EARLY:])
 
         nc.scalar.activation(gated[:], gates[:].indirect(offsets[:]), SILU)
+        nc.vector.tensor_copy(stream[:, FIRST:EARLY], landed[:, FIRST:])
 
-        look_up(0, EARLY)
-        look_up(EARLY, HALF)
-        look_up(HALF, PICKS - LAST)
-        multiply(0, HALF)
-        store(0, HALF)
-        look_up(PICKS - LAST, PICKS)
-        multiply(HALF, PICKS - LAST)
-        multiply(PICKS - LAST, PICKS)
-        store(HALF, PICKS)
+        look_up(0, FIRST, landed)
+        look_up(PICKS - QUARTER, PICKS, stream)
+        look_up(FIRST, PICKS - QUARTER, stream)
+        for part in (outer, middle):
+            nc.vector.tensor_tensor(part(product[:]), part(lesser[:]), part(gated[:]), MULT)
+            nc.sync.dma_start(part(out), part(product[:]))

@@ -15,6 +15,7 @@ DMA_ALIGN = 4096
 QUARTER = PICKS // 4
 EARLY = 192
 FIRST = 160
+PIECE_BYTES = 256
 
 
 def tile_lookup_vg_minsilu_out_kernel(tc, tab, y, offs, out):
@@ -40,7 +41,7 @@ def tile_lookup_vg_minsilu_out_kernel(tc, tab, y, offs, out):
             return rows[:, QUARTER : PICKS - QUARTER]
 
         nc.sync.dma_start(gates[:], tab[1])
-        nc.scalar.dma_start(landed[:], y[:, :EARLY])
+        nc.scalar.dma_start(landed[:], y[:, :EARLY], max_dma_last_dim=PIECE_BYTES)
         nc.scalar.dma_start(values[:], tab[0])
         nc.sync.dma_start(offsets[:], offs)
         nc.scalar.dma_start(stream[:, EARLY:], y[:, EARLY:])

import concourse.mybir as mybir

F32 = mybir.dt.float32
U16 = mybir.dt.uint16
MIN = mybir.AluOpType.min
MULT = mybir.AluOpType.mult
SILU = mybir.ActivationFunctionType.Silu

ROWS, PLACES, PICKS = 128, 2048, 512
PER_COLUMN = 16

FLOPS = 6 * ROWS * PICKS
DMA_ALIGN = 4096

QUARTER = PICKS // 4
EARLY = 192
FIRST = 160
PIECE_BYTES = 256


def tile_lookup_vg_minsilu_out_kernel(tc, tab, y, offs, out):
    nc = tc.nc
    with tc.tile_pool(name="held", bufs=1) as held:
        offsets = held.tile([ROWS, PICKS // PER_COLUMN], U16, name="offsets", align_bytes=DMA_ALIGN)
        gates = held.tile([ROWS, PLACES], F32, name="gates", align_bytes=DMA_ALIGN)
        values = held.tile([ROWS, PLACES], F32, name="values", align_bytes=DMA_ALIGN)
        stream = held.tile([ROWS, PICKS], F32, name="stream", align_bytes=DMA_ALIGN)
        landed = held.tile([ROWS, EARLY], F32, name="landed", align_bytes=DMA_ALIGN)
        gated = held.tile([ROWS, PICKS], F32, name="gated")
        lesser = held.tile([ROWS, PICKS], F32, name="lesser")
        product = held.tile([ROWS, PICKS], F32, name="product", align_bytes=DMA_ALIGN)

        def look_up(first, last, columns):
            piece_offsets = offsets[:, first // PER_COLUMN : last // PER_COLUMN]
            nc.vector.tensor_tensor(lesser[:, first:last], values[:].indirect(piece_offsets), columns[:, first:last], MIN)

        def outer(rows):
            return rows.rearrange("p (q c) -> p q c", c=QUARTER)[:, ::3, :]

        def middle(rows):
            return rows[:, QUARTER : PICKS - QUARTER]

        nc.sync.dma_start(gates[:], tab[1])
        nc.scalar.dma_start(landed[:], y[:, :EARLY], max_dma_last_dim=PIECE_BYTES)
        nc.scalar.dma_start(values[:], tab[0])
        nc.sync.dma_start(offsets[:], offs)
        nc.scalar.dma_start(stream[:, EARLY:], y[:, EARLY:])

        nc.scalar.activation(gated[:], gates[:].indirect(offsets[:]), SILU)
        nc.vector.tensor_copy(stream[:, FIRST:EARLY], landed[:, FIRST:])

        look_up(0, FIRST, landed)
        look_up(PICKS - QUARTER, PICKS, stream)
        look_up(FIRST, PICKS - QUARTER, stream)
        for part in (outer, middle):
            nc.vector.tensor_tensor(part(product[:]), part(lesser[:]), part(gated[:]), MULT)
            nc.sync.dma_start(part(out), part(product[:]))
